import numpy as np
import ml_dtypes


def mxq(x, axis, fmt="e4m3"):
    dtype, down = {"e4m3": (ml_dtypes.float8_e4m3fn, 7), "e5m2": (ml_dtypes.float8_e5m2, 14)}[fmt]
    v = np.moveaxis(np.asarray(x, np.float32).astype(ml_dtypes.bfloat16).astype(np.float64), axis, -1)
    blocks = v.reshape(v.shape[:-1] + (-1, 32))
    amax = np.abs(blocks).max(-1, keepdims=True)
    byte = np.maximum(np.where(amax > 0, np.frexp(amax)[1] - 1 + 127, 0) - down, 1)
    scale = np.exp2(byte - 127.0)
    codes = (blocks / scale).astype(np.float32).astype(dtype).astype(np.float64)
    return np.moveaxis((codes * scale).reshape(v.shape), -1, axis)


WIDE = False


def mx_kscale(k):
    if not WIDE:
        return np.ones(k)
    levels = np.array([10, -10, 5, -5, 0])
    if k % 512:
        return np.exp2(np.random.permutation(np.resize(levels, k // 32))).repeat(32)
    a = np.empty((k // 512, 16))
    for p in range(k // 512):
        a[p, :8] = np.random.permutation(np.resize(levels, 8))
        for g in range(8):
            far = levels[np.abs(levels - a[p, g]) >= 10]
            a[p, g + 8] = far[np.random.randint(len(far))]
    return np.exp2(a.ravel()).repeat(32)


def f64(x):
    return np.asarray(x).astype(np.float64)


def striped(idx):
    return np.tile(np.asarray(idx).reshape(-1, 16).T, (8, 1)).astype(np.uint16)


def unstriped(offs):
    return offs[:16].T.reshape(-1).astype(np.int64)


E2M1 = np.array([0.0, 0.5, 1.0, 1.5, 2.0, 3.0, 4.0, 6.0, -0.0, -0.5, -1.0, -1.5, -2.0, -3.0, -4.0, -6.0])


def pack_weight(w, fmt):
    k, n = w.shape
    w = f64(np.asarray(w, np.float32).astype(ml_dtypes.bfloat16)).reshape(k // 32, 32, n)
    amax = np.abs(w).max(1)
    if fmt == "e4m3":
        byte = np.frexp(amax)[1] - 1 + 127 - 7
    else:
        mant, ex = np.frexp(amax / 6.0)
        byte = np.where(mant > 0.5, ex, ex - 1) + 127
    byte = np.clip(np.where(amax > 0, byte, 1), 1, 254)
    scaled = (w * np.exp2(127.0 - byte)[:, None, :]).reshape(k, n).astype(np.float32)
    by_word = np.ascontiguousarray(scaled.reshape(k // 512, 128, 4, n).transpose(0, 1, 3, 2))
    if fmt == "e4m3":
        words = by_word.astype(ml_dtypes.float8_e4m3fn).view(np.uint8)
    else:
        c = by_word.astype(ml_dtypes.float4_e2m1fn).view(np.uint8) & 0xF
        words = (c[..., 0::2] | (c[..., 1::2] << 4)).reshape(k // 512, 128, 2 * n)
    return np.ascontiguousarray(words), np.ascontiguousarray(byte.astype(np.uint8).reshape(k // 512, 16, n))


def unpack_weight(words, scales, fmt):
    g, _, n = scales.shape
    words = np.ascontiguousarray(words).reshape(g, 128, n, -1)
    if fmt == "e4m3":
        vals = words.view(ml_dtypes.float8_e4m3fn).astype(np.float64)
    else:
        nib = np.empty((g, 128, n, 4), np.uint8)
        nib[..., 0::2] = words & 0xF
        nib[..., 1::2] = words >> 4
        vals = E2M1[nib]
    vals = vals * np.repeat(np.exp2(scales.astype(np.float64) - 127.0), 8, axis=1)[..., None]
    return vals.transpose(0, 1, 3, 2).reshape(g * 512, n)


D, T, I, Q, X = 1024, 4096, 1024, 512, 64


def setup_inputs():
    n = np.random.standard_normal
    idx = np.random.permutation(T)[:I]
    fd = mx_kscale(D)
    vocp = pack_weight(n((D, T)) / fd[:, None], "e2m1")
    return {
        "hid": (n((D, Q)) * 1.0 / np.sqrt(D) * fd[:, None]).astype(np.float32),
        "voc_words": vocp[0],
        "voc_scales": vocp[1],
        "pd": (np.random.uniform(0.05, 0.2, (Q, 1))).astype(np.float32),
        "offs": striped(idx),
    }


def reference(hid, voc_words, voc_scales, pd, offs):
    idx = unstriped(offs)
    vocu = unpack_weight(voc_words, voc_scales, "e2m1")
    hidq = mxq(f64(hid), 0, "e4m3")
    vocidxg = vocu[:, idx]
    a = hidq.T @ vocidxg
    p = np.exp(a - np.max(a, axis=1, keepdims=True))
    w = p * f64(pd) / np.sum(p, axis=1, keepdims=True)
    wt = w.T
    y = wt.reshape(I, X, Q // X).sum(axis=2) * 512.0
    return y

from contextlib import ExitStack

import concourse.mybir as mybir

D, T, I, Q, X = 1024, 4096, 1024, 512, 64
FLOPS = 2 * D * I * Q

F32 = mybir.dt.float32
BF16 = mybir.dt.bfloat16
I32 = mybir.dt.int32
U32 = mybir.dt.uint32
U16 = mybir.dt.uint16
U8 = mybir.dt.uint8
FP8X4 = mybir.dt.float8_e4m3fn_x4
FP4X4 = mybir.dt.float4_e2m1fn_x4
ALU = mybir.AluOpType
ACT = mybir.ActivationFunctionType
AX = mybir.AxisListType

P = 128
PACK = 4
PASSES = D // (P * PACK)
BANK = 512
HALVES = 2
QH = Q // HALVES
XH = X // HALVES


def tile_attend_ragmarginal_kernel(tc, hid, voc_words, voc_scales, pd, offs, out):
    nc = tc.nc
    with ExitStack() as ctx:
        keep = ctx.enter_context(tc.tile_pool(name="keep", bufs=1))
        shared = ctx.enter_context(tc.tile_pool(name="shared", bufs=1))
        psum = ctx.enter_context(tc.psum_pool(name="psum", bufs=1))

        offsets = keep.tile([P, I // 16], U16, name="offsets")
        nc.sync.dma_start(offsets[:], offs)

        pd_t = keep.tile([P, HALVES, 2], F32, name="pd_t", tag="raw")
        nc.sync.dma_start(out=pd_t[:], in_=pd.rearrange("(h m u) o -> m h (u o)", h=HALVES, u=2))

        scale_win = shared.tile([P, T], U8, name="scale_win", offset=0, align_bytes=64)
        nc.vector.memset(scale_win[:].bitcast(I32), 0)
        for z in range(PASSES):
            nc.scalar.dma_start(out=scale_win[4 * z : P : 8, :].bitcast(I32), in_=voc_scales[z].bitcast(I32))

        ones = keep.tile([P, P], F32, name="ones")
        nc.vector.memset(ones[:], 1.0)
        ident = keep.tile([P, P], F32, name="ident")
        nc.gpsimd.affine_select(
            out=ident[:], in_=ones[:], compare_op=ALU.is_equal, fill=0.0, base=0, pattern=[[-1, P]], channel_multiplier=1
        )
        warm = keep.tile([P, 1], F32, name="warm", tag="word_win1", align_bytes=64)
        nc.vector.memset(warm[:], 0.0)
        warm2 = keep.tile([P, 1], F32, name="warm2")
        nc.scalar.activation(out=warm2[:], in_=warm[:], func=ACT.Exp)

        pd512 = keep.tile([P, HALVES * 2], F32, name="pd512")
        nc.vector.tensor_scalar(
            out=pd512[:], in0=pd_t[:].rearrange("p h u -> p (h u)"), scalar1=512.0, scalar2=None, op0=ALU.mult
        )

        word_win = []
        for z in range(PASSES):
            win = keep.tile([P, T], U16, name=f"word_win{z}", tag=f"word_win{z}", align_bytes=64)
            nc.sync.dma_start(out=win[:].bitcast(I32), in_=voc_words[z].bitcast(I32))
            word_win.append(win)

        raw = {}

        def load_hid(hf, tile):
            raw[hf] = tile
            for z in range(PASSES):
                rows = hid[512 * z : 512 * (z + 1), QH * hf : QH * (hf + 1)]
                nc.sync.dma_start(out=tile[:, z], in_=rows.rearrange("(p j) q -> p j q", j=PACK))

        load_hid(0, keep.tile([P, PASSES, PACK, QH], F32, name="raw0", tag="raw"))

        planes = keep.tile([P, PASSES, I], U8, name="planes", align_bytes=64)
        nc.gpsimd.memset(planes[:].rearrange("p z i -> p (z i)").bitcast(I32), 0)

        picked = keep.tile([P, I], U8, name="picked", align_bytes=64)
        nc.vector.tensor_copy(picked[:], scale_win[:].indirect(offsets[:]))
        for quad in range(4):
            nc.sync.dma_start(
                out=planes[32 * quad : 32 * quad + 4].rearrange("p z i -> p (z i)").bitcast(I32),
                in_=picked[32 * quad : 32 * quad + 32 : 4, :].bitcast(I32),
            )

        load_hid(1, shared.tile([P, PASSES, PACK, QH], F32, name="raw1", offset=2 * I, align_bytes=64))

        words = [
            shared.tile([P, I], U16, name="words0", offset=0, align_bytes=64),
            keep.tile([P, I], U16, name="words1", align_bytes=64),
        ]

        def gather_words(z, lo, hi):
            nc.vector.tensor_copy(words[z][:, lo:hi], word_win[z][:].indirect(offsets[:, lo // 16 : hi // 16]))

        gather_words(0, 0, I)

        codes, hscale, grouped = {}, {}, {}

        def interleave(hf, z):
            grouped[hf, z] = keep.tile([P, 2, P, PACK], BF16, name=f"grouped{hf}{z}", tag=f"grouped{hf}{z}", align_bytes=64)
            nc.scalar.copy(
                out=grouped[hf, z][:].rearrange("p u (c m) j -> p c j m u", m=2),
                in_=raw[hf][:, z].rearrange("p j (c m u) -> p c j m u", m=2, u=2),
            )

        def quantize(hf, z):
            c = keep.tile([P, QH], U32, name=f"codes{hf}{z}", align_bytes=64)
            s = keep.tile([P, QH], U8, name=f"hscale{hf}{z}", align_bytes=64)
            nc.vector.quantize_mx(
                out=c[:].bitcast(FP8X4), scales=s[:], in_=grouped[hf, z][:].rearrange("p u m j -> p (u m j)")
            )
            codes[hf, z], hscale[hf, z] = c, s

        score = {}

        def scores(t):
            hf, u = divmod(t, 2)
            cols = slice(P * u, P * (u + 1))
            for h in range(2):
                acc = psum.tile([P, BANK], F32, name=f"score{t}{h}", tag=f"bank{2 * t + h}")
                icols = slice(BANK * h, BANK * (h + 1))
                for z in range(PASSES):
                    nc.tensor.matmul_mx(
                        out=acc[:],
                        lhsT=codes[hf, z][:, cols].bitcast(FP8X4),
                        lhsT_scale=hscale[hf, z][:, cols],
                        rhs=words[z][:, icols].bitcast(FP4X4),
                        rhs_scale=planes[:, z, icols],
                        start=(z == 0),
                        stop=(z == PASSES - 1),
                    )
                score[t, h] = acc

        prob, stats = {}, {}

        def softmax(t):
            nm2 = keep.tile([P, 2], F32, name=f"nm2{t}", tag=("grouped10", "grouped11", "nm22", "nm23")[t], align_bytes=64)
            part = [keep.tile([P, 1], F32, name=f"part{t}{h}") for h in range(2)]
            pr = [
                shared.tile([P, 4, P], F32, name="prob00", offset=4 * I, align_bytes=64)
                if t + h == 0
                else keep.tile([P, 4, P], F32, name=f"prob{t}{h}")
                for h in range(2)
            ]
            for h in range(2):
                nc.vector.tensor_reduce(out=nm2[:, h : h + 1], in_=score[t, h][:], axis=AX.X, op=ALU.max, negate=True)
            negtop = keep.tile([P, 1], F32, name=f"negtop{t}")
            nc.vector.tensor_reduce(out=negtop[:], in_=nm2[:], axis=AX.X, op=ALU.min)
            fac = keep.tile([P, 2], F32, name=f"fac{t}")
            first = keep.tile([P, 1], F32, name=f"first{t}")
            gain = keep.tile([P, 2], F32, name=f"gain{t}")
            total = keep.tile([P, 1], F32, name=f"total{t}")
            rinv = keep.tile([P, 1], F32, name=f"rinv{t}")

            def expo(h):
                nc.scalar.activation(
                    out=pr[h][:],
                    in_=score[t, h][:].rearrange("p (a b) -> p b a", b=4),
                    func=ACT.Exp,
                    bias=nm2[:, h : h + 1],
                    accum_out=part[h][:],
                )

            expo(0)
            nc.scalar.activation(out=fac[:], in_=nm2[:], func=ACT.Exp, bias=negtop[:], scale=-1.0)
            expo(1)
            nc.scalar.activation(out=gain[:], in_=fac[:], func=ACT.Copy, scale=pd512[:, t : t + 1])
            nc.vector.tensor_scalar(out=first[:], in0=part[0][:], scalar1=fac[:, 0:1], scalar2=None, op0=ALU.mult)
            nc.vector.tensor_scalar(
                out=total[:], in0=part[1][:], scalar1=fac[:, 1:2], scalar2=first[:], op0=ALU.mult, op1=ALU.add
            )
            nc.vector.reciprocal(out=rinv[:], in_=total[:])
            prob[t], stats[t] = pr, (gain, rinv)

        turned = {}

        def weigh(t, engs):
            hf, u = divmod(t, 2)
            gain, rinv = stats[t]
            for h in range(2):
                w = keep.tile([P, 4, P], F32, name=f"weight{t}{h}")
                engs[h].tensor_scalar(
                    out=w[:], in0=prob[t][h][:], scalar1=gain[:, h : h + 1], scalar2=rinv[:], op0=ALU.mult, op1=ALU.mult
                )
                if u == 0:
                    turned[hf, h] = psum.tile([P, 4, P], F32, name=f"turned{hf}{h}", tag=f"bank{2 * hf + h}")
                for b in range(4):
                    nc.tensor.matmul(
                        out=turned[hf, h][:, b, :],
                        lhsT=w[:, b, :],
                        rhs=ident[:],
                        is_transpose=True,
                        start=(u == 0 and b == 0),
                        stop=(u == 1 and b == 3),
                    )

        stage = [keep.tile([P, 4, X], F32, name=f"stage{h}") for h in range(2)]

        def fold(hf, h):
            nc.vector.tensor_reduce(
                out=stage[h][:, :, XH * hf : XH * (hf + 1)],
                in_=turned[hf, h][:].rearrange("p b (x e) -> p b x e", e=4),
                axis=AX.X,
                op=ALU.add,
            )

        for hf in range(HALVES):
            for z in range(PASSES):
                interleave(hf, z)
        quantize(0, 0)
        quantize(0, 1)
        gather_words(1, 0, BANK)
        gather_words(1, BANK, I)
        scores(0)
        scores(1)
        quantize(1, 0)
        softmax(0)
        quantize(1, 1)
        scores(2)
        scores(3)
        softmax(1)
        weigh(0, (nc.gpsimd, nc.gpsimd))
        softmax(2)
        weigh(1, (nc.gpsimd, nc.vector))
        softmax(3)
        weigh(2, (nc.vector, nc.vector))
        weigh(3, (nc.vector, nc.vector))
        fold(0, 0)
        fold(0, 1)
        for h in range(2):
            fold(1, h)
            nc.sync.dma_start(
                out=out[BANK * h : BANK * (h + 1), :].rearrange("(a b) x -> a b x", b=4), in_=stage[h][:]
            )
